import numpy as np
import ml_dtypes

BF16 = ml_dtypes.bfloat16


def bf(x):
    return np.asarray(x, np.float32).astype(BF16)


def f32(x):
    return np.asarray(x, np.float32)


def f64(x):
    return np.asarray(x).astype(np.float64)


def striped(idx):
    return np.tile(idx.reshape(-1, 16).T, (8, 1))


def rows(idx, k):
    return np.tile(idx, (k, 1))


def look(tab, idx):
    return np.take_along_axis(f64(tab), rows(idx, len(tab)), axis=1)


K, S, V, N, M = 128, 2048, 2048, 2048, 128


def setup_inputs():
    return {"tab": f32(np.random.standard_normal((K, S))), "qry": f32(1.0 * np.random.standard_normal((K, V))), "w": bf(np.random.uniform(0.0, 2.0, (K, M)) / K), "offs": striped(np.random.permutation(S)[:N])}


def reference(tab, qry, w, offs):
    idx = offs[:16].T.reshape(-1)
    a = f64(w).T @ (look(tab, idx) * f64(qry))
    b = f64(w).T @ look(tab, idx) ** 2
    return a / np.sqrt(b + 0.01)

@@ -1,0 +1,57 @@
+import concourse.mybir as mybir
+
+F32, BF16, U16 = mybir.dt.float32, mybir.dt.bfloat16, mybir.dt.uint16
+MULT = mybir.AluOpType.mult
+ACT = mybir.ActivationFunctionType
+
+ROWS, COLUMNS, N, M = 128, 2048, 2048, 128
+PIECE = 512
+OFFSETS_PER_COLUMN = 16
+FLOPS = 2 * 2 * ROWS * M * N
+
+
+def tile_lookup_cosine_cos_kernel(tc, tab, qry, w, offs, out):
+    nc = tc.nc
+    with (
+        tc.tile_pool(name="held", bufs=1) as held,
+        tc.tile_pool(name="work", bufs=4) as work,
+        tc.psum_pool(name="psum", bufs=4) as psum,
+    ):
+        offsets = held.tile([ROWS, N // OFFSETS_PER_COLUMN], U16, name="offsets")
+        nc.sync.dma_start(offsets[:], offs)
+        table = held.tile([ROWS, COLUMNS], F32, name="table")
+        nc.sync.dma_start(table[:], tab)
+        queries = held.tile([ROWS, N], F32, name="queries")
+        weights = held.tile([ROWS, M], BF16, name="weights")
+        for first in range(0, N, PIECE):
+            nc.sync.dma_start(queries[:, first : first + PIECE], qry[:, first : first + PIECE])
+            if first == 0:
+                nc.sync.dma_start(weights[:], w)
+
+        epsilon = held.tile([M, 1], F32, name="epsilon")
+        nc.vector.memset(epsilon[:], 0.01)
+        weights_f32 = held.tile([ROWS, M], F32, name="weights_f32")
+        nc.vector.tensor_copy(weights_f32[:], weights[:])
+
+        for first in range(0, N, PIECE):
+            columns = slice(first, first + PIECE)
+            looked_up = table[:].indirect(
+                offsets[:, first // OFFSETS_PER_COLUMN : (first + PIECE) // OFFSETS_PER_COLUMN]
+            )
+            squares = work.tile([ROWS, PIECE], F32, name="squares")
+            nc.scalar.activation(squares[:], looked_up, ACT.Square)
+            products = work.tile([ROWS, PIECE], F32, name="products")
+            nc.vector.tensor_tensor(products[:], looked_up, queries[:, columns], MULT)
+            products_bf16 = work.tile([ROWS, PIECE], BF16, name="products_bf16")
+            nc.vector.tensor_copy(products_bf16[:], products[:])
+
+            b = psum.tile([M, PIECE], F32, name="b")
+            nc.tensor.matmul(b[:], weights_f32[:], squares[:], start=True, stop=True)
+            a = psum.tile([M, PIECE], F32, name="a")
+            nc.tensor.matmul(a[:], weights[:], products_bf16[:], start=True, stop=True)
+
+            inverse_norm = work.tile([M, PIECE], F32, name="inverse_norm")
+            nc.scalar.activation(inverse_norm[:], b[:], ACT.Abs_reciprocal_sqrt, bias=epsilon[:])
+            result = work.tile([M, PIECE], F32, name="result")
+            nc.vector.tensor_tensor(result[:], a[:], inverse_norm[:], MULT)
+            nc.sync.dma_start(out[:, columns], result[:])

@@ -5,8 +5,10 @@ MULT = mybir.AluOpType.mult
 ACT = mybir.ActivationFunctionType
 
 ROWS, COLUMNS, N, M = 128, 2048, 2048, 128
-PIECE = 512
+BANK = 512
+PIECES = [512, 512, 512, 256, 256]
 OFFSETS_PER_COLUMN = 16
+WARM_UP_MATMULS = 10
 FLOPS = 2 * 2 * ROWS * M * N
 
 
@@ -15,43 +17,59 @@ def tile_lookup_cosine_cos_kernel(tc, tab, qry, w, offs, out):
     with (
         tc.tile_pool(name="held", bufs=1) as held,
         tc.tile_pool(name="work", bufs=4) as work,
-        tc.psum_pool(name="psum", bufs=4) as psum,
+        tc.psum_pool(name="psum", bufs=3) as psum,
+        tc.psum_pool(name="warm_up_psum", bufs=1) as warm_up_psum,
     ):
         offsets = held.tile([ROWS, N // OFFSETS_PER_COLUMN], U16, name="offsets")
         nc.sync.dma_start(offsets[:], offs)
+        weights = held.tile([ROWS, M], BF16, name="weights")
+        nc.scalar.dma_start(weights[:], w)
         table = held.tile([ROWS, COLUMNS], F32, name="table")
         nc.sync.dma_start(table[:], tab)
         queries = held.tile([ROWS, N], F32, name="queries")
-        weights = held.tile([ROWS, M], BF16, name="weights")
-        for first in range(0, N, PIECE):
-            nc.sync.dma_start(queries[:, first : first + PIECE], qry[:, first : first + PIECE])
-            if first == 0:
-                nc.sync.dma_start(weights[:], w)
+        first = 0
+        for piece in PIECES:
+            nc.sync.dma_start(queries[:, first : first + piece], qry[:, first : first + piece])
+            first += piece
+
+        zeros = held.tile([ROWS, BANK], BF16, name="zeros")
+        nc.gpsimd.memset(zeros[:], 0.0)
+        idle_bank = warm_up_psum.tile([M, BANK], F32, name="idle_bank")
+        for turn in range(WARM_UP_MATMULS):
+            nc.tensor.matmul(idle_bank[:], zeros[:, :M], zeros[:], start=True, stop=True)
 
         epsilon = held.tile([M, 1], F32, name="epsilon")
         nc.vector.memset(epsilon[:], 0.01)
+        warm_up = held.tile([M, 1], F32, name="warm_up")
+        nc.scalar.activation(warm_up[:], epsilon[:], ACT.Abs_reciprocal_sqrt)
         weights_f32 = held.tile([ROWS, M], F32, name="weights_f32")
         nc.vector.tensor_copy(weights_f32[:], weights[:])
 
-        for first in range(0, N, PIECE):
-            columns = slice(first, first + PIECE)
-            looked_up = table[:].indirect(
-                offsets[:, first // OFFSETS_PER_COLUMN : (first + PIECE) // OFFSETS_PER_COLUMN]
-            )
-            squares = work.tile([ROWS, PIECE], F32, name="squares")
-            nc.scalar.activation(squares[:], looked_up, ACT.Square)
-            products = work.tile([ROWS, PIECE], F32, name="products")
-            nc.vector.tensor_tensor(products[:], looked_up, queries[:, columns], MULT)
-            products_bf16 = work.tile([ROWS, PIECE], BF16, name="products_bf16")
-            nc.vector.tensor_copy(products_bf16[:], products[:])
-
-            b = psum.tile([M, PIECE], F32, name="b")
-            nc.tensor.matmul(b[:], weights_f32[:], squares[:], start=True, stop=True)
-            a = psum.tile([M, PIECE], F32, name="a")
-            nc.tensor.matmul(a[:], weights[:], products_bf16[:], start=True, stop=True)
-
-            inverse_norm = work.tile([M, PIECE], F32, name="inverse_norm")
+        def finish(first, piece, a, b):
+            inverse_norm = work.tile([M, piece], F32, name="inverse_norm")
             nc.scalar.activation(inverse_norm[:], b[:], ACT.Abs_reciprocal_sqrt, bias=epsilon[:])
-            result = work.tile([M, PIECE], F32, name="result")
+            result = work.tile([M, piece], F32, name="result")
             nc.vector.tensor_tensor(result[:], a[:], inverse_norm[:], MULT)
-            nc.sync.dma_start(out[:, columns], result[:])
+            nc.sync.dma_start(out[:, first : first + piece], result[:])
+
+        waiting = []
+        first = 0
+        for piece in PIECES:
+            looked_up = table[:].indirect(
+                offsets[:, first // OFFSETS_PER_COLUMN : (first + piece) // OFFSETS_PER_COLUMN]
+            )
+            squares = work.tile([ROWS, piece], F32, name="squares")
+            nc.scalar.activation(squares[:], looked_up, ACT.Square)
+            products = work.tile([ROWS, piece], F32, name="products")
+            nc.vector.tensor_tensor(products[:], looked_up, queries[:, first : first + piece], MULT)
+            b = psum.tile([M, piece], F32, name="b")
+            nc.tensor.matmul(b[:], weights_f32[:], squares[:], start=True, stop=True)
+            a = psum.tile([M, piece], F32, name="a")
+            products_bf16 = work.tile([ROWS, piece], BF16, name="products_bf16")
+            nc.vector.tensor_copy(products_bf16[:], products[:])
+            nc.tensor.matmul(a[:], weights[:], products_bf16[:], start=True, stop=True)
+            waiting.append((first, piece, a, b))
+            if len(waiting) > 1:
+                finish(*waiting.pop(0))
+            first += piece
+        finish(*waiting.pop(0))

@@ -8,7 +8,7 @@ ROWS, COLUMNS, N, M = 128, 2048, 2048, 128
 BANK = 512
 PIECES = [512, 512, 512, 256, 256]
 OFFSETS_PER_COLUMN = 16
-WARM_UP_MATMULS = 10
+WARM_UP_MATMULS = 14
 FLOPS = 2 * 2 * ROWS * M * N
 
 
@@ -65,9 +65,12 @@ def tile_lookup_cosine_cos_kernel(tc, tab, qry, w, offs, out):
             b = psum.tile([M, piece], F32, name="b")
             nc.tensor.matmul(b[:], weights_f32[:], squares[:], start=True, stop=True)
             a = psum.tile([M, piece], F32, name="a")
-            products_bf16 = work.tile([ROWS, piece], BF16, name="products_bf16")
-            nc.vector.tensor_copy(products_bf16[:], products[:])
-            nc.tensor.matmul(a[:], weights[:], products_bf16[:], start=True, stop=True)
+            if first == 0:
+                nc.tensor.matmul(a[:], weights_f32[:], products[:], start=True, stop=True)
+            else:
+                products_bf16 = work.tile([ROWS, piece], BF16, name="products_bf16")
+                nc.vector.tensor_copy(products_bf16[:], products[:])
+                nc.tensor.matmul(a[:], weights[:], products_bf16[:], start=True, stop=True)
             waiting.append((first, piece, a, b))
             if len(waiting) > 1:
                 finish(*waiting.pop(0))

import concourse.mybir as mybir

F32, BF16, U16 = mybir.dt.float32, mybir.dt.bfloat16, mybir.dt.uint16
MULT = mybir.AluOpType.mult
ACT = mybir.ActivationFunctionType

ROWS, COLUMNS, N, M = 128, 2048, 2048, 128
BANK = 512
PIECES = [512, 512, 512, 256, 256]
OFFSETS_PER_COLUMN = 16
WARM_UP_MATMULS = 14
FLOPS = 2 * 2 * ROWS * M * N


def tile_lookup_cosine_cos_kernel(tc, tab, qry, w, offs, out):
    nc = tc.nc
    with (
        tc.tile_pool(name="held", bufs=1) as held,
        tc.tile_pool(name="work", bufs=4) as work,
        tc.psum_pool(name="psum", bufs=3) as psum,
        tc.psum_pool(name="warm_up_psum", bufs=1) as warm_up_psum,
    ):
        offsets = held.tile([ROWS, N // OFFSETS_PER_COLUMN], U16, name="offsets")
        nc.sync.dma_start(offsets[:], offs)
        weights = held.tile([ROWS, M], BF16, name="weights")
        nc.scalar.dma_start(weights[:], w)
        table = held.tile([ROWS, COLUMNS], F32, name="table")
        nc.sync.dma_start(table[:], tab)
        queries = held.tile([ROWS, N], F32, name="queries")
        first = 0
        for piece in PIECES:
            nc.sync.dma_start(queries[:, first : first + piece], qry[:, first : first + piece])
            first += piece

        zeros = held.tile([ROWS, BANK], BF16, name="zeros")
        nc.gpsimd.memset(zeros[:], 0.0)
        idle_bank = warm_up_psum.tile([M, BANK], F32, name="idle_bank")
        for turn in range(WARM_UP_MATMULS):
            nc.tensor.matmul(idle_bank[:], zeros[:, :M], zeros[:], start=True, stop=True)

        epsilon = held.tile([M, 1], F32, name="epsilon")
        nc.vector.memset(epsilon[:], 0.01)
        warm_up = held.tile([M, 1], F32, name="warm_up")
        nc.scalar.activation(warm_up[:], epsilon[:], ACT.Abs_reciprocal_sqrt)
        weights_f32 = held.tile([ROWS, M], F32, name="weights_f32")
        nc.vector.tensor_copy(weights_f32[:], weights[:])

        def finish(first, piece, a, b):
            inverse_norm = work.tile([M, piece], F32, name="inverse_norm")
            nc.scalar.activation(inverse_norm[:], b[:], ACT.Abs_reciprocal_sqrt, bias=epsilon[:])
            result = work.tile([M, piece], F32, name="result")
            nc.vector.tensor_tensor(result[:], a[:], inverse_norm[:], MULT)
            nc.sync.dma_start(out[:, first : first + piece], result[:])

        waiting = []
        first = 0
        for piece in PIECES:
            looked_up = table[:].indirect(
                offsets[:, first // OFFSETS_PER_COLUMN : (first + piece) // OFFSETS_PER_COLUMN]
            )
            squares = work.tile([ROWS, piece], F32, name="squares")
            nc.scalar.activation(squares[:], looked_up, ACT.Square)
            products = work.tile([ROWS, piece], F32, name="products")
            nc.vector.tensor_tensor(products[:], looked_up, queries[:, first : first + piece], MULT)
            b = psum.tile([M, piece], F32, name="b")
            nc.tensor.matmul(b[:], weights_f32[:], squares[:], start=True, stop=True)
            a = psum.tile([M, piece], F32, name="a")
            if first == 0:
                nc.tensor.matmul(a[:], weights_f32[:], products[:], start=True, stop=True)
            else:
                products_bf16 = work.tile([ROWS, piece], BF16, name="products_bf16")
                nc.vector.tensor_copy(products_bf16[:], products[:])
                nc.tensor.matmul(a[:], weights[:], products_bf16[:], start=True, stop=True)
            waiting.append((first, piece, a, b))
            if len(waiting) > 1:
                finish(*waiting.pop(0))
            first += piece
        finish(*waiting.pop(0))
